import numpy as np
import ml_dtypes


def mxq(x, axis, fmt="e4m3"):
    dtype, down = {"e4m3": (ml_dtypes.float8_e4m3fn, 7), "e5m2": (ml_dtypes.float8_e5m2, 14)}[fmt]
    v = np.moveaxis(np.asarray(x, np.float32).astype(ml_dtypes.bfloat16).astype(np.float64), axis, -1)
    blocks = v.reshape(v.shape[:-1] + (-1, 32))
    amax = np.abs(blocks).max(-1, keepdims=True)
    byte = np.maximum(np.where(amax > 0, np.frexp(amax)[1] - 1 + 127, 0) - down, 1)
    scale = np.exp2(byte - 127.0)
    codes = (blocks / scale).astype(np.float32).astype(dtype).astype(np.float64)
    return np.moveaxis((codes * scale).reshape(v.shape), -1, axis)


WIDE = False


def mx_kscale(k):
    if not WIDE:
        return np.ones(k)
    levels = np.array([10, -10, 5, -5, 0])
    if k % 512:
        return np.exp2(np.random.permutation(np.resize(levels, k // 32))).repeat(32)
    a = np.empty((k // 512, 16))
    for p in range(k // 512):
        a[p, :8] = np.random.permutation(np.resize(levels, 8))
        for g in range(8):
            far = levels[np.abs(levels - a[p, g]) >= 10]
            a[p, g + 8] = far[np.random.randint(len(far))]
    return np.exp2(a.ravel()).repeat(32)


BF16 = ml_dtypes.bfloat16


def bf(x):
    return np.asarray(x, np.float32).astype(BF16)


def f64(x):
    return np.asarray(x).astype(np.float64)


E2M1 = np.array([0.0, 0.5, 1.0, 1.5, 2.0, 3.0, 4.0, 6.0, -0.0, -0.5, -1.0, -1.5, -2.0, -3.0, -4.0, -6.0])


def pack_weight(w, fmt):
    k, n = w.shape
    w = f64(bf(w)).reshape(k // 32, 32, n)
    amax = np.abs(w).max(1)
    if fmt == "e4m3":
        byte = np.frexp(amax)[1] - 1 + 127 - 7
    else:
        mant, ex = np.frexp(amax / 6.0)
        byte = np.where(mant > 0.5, ex, ex - 1) + 127
    byte = np.clip(np.where(amax > 0, byte, 1), 1, 254)
    scaled = (w * np.exp2(127.0 - byte)[:, None, :]).reshape(k, n).astype(np.float32)
    by_word = np.ascontiguousarray(scaled.reshape(k // 512, 128, 4, n).transpose(0, 1, 3, 2))
    if fmt == "e4m3":
        words = by_word.astype(ml_dtypes.float8_e4m3fn).view(np.uint8)
    else:
        c = by_word.astype(ml_dtypes.float4_e2m1fn).view(np.uint8) & 0xF
        words = c[..., 0::2] | (c[..., 1::2] << 4)
    return np.ascontiguousarray(words), np.ascontiguousarray(byte.astype(np.uint8).reshape(k // 512, 16, n))


def unpack_weight(words, scales, fmt):
    g, p, n, _ = words.shape
    if fmt == "e4m3":
        vals = np.ascontiguousarray(words).view(ml_dtypes.float8_e4m3fn).astype(np.float64)
    else:
        nib = np.empty((g, p, n, 4), np.uint8)
        nib[..., 0::2] = words & 0xF
        nib[..., 1::2] = words >> 4
        vals = E2M1[nib]
    vals = vals * np.repeat(np.exp2(scales.astype(np.float64) - 127.0), 8, axis=1)[..., None]
    return vals.transpose(0, 1, 3, 2).reshape(g * 512, n)

E4M3FN = np.array([(-1.0 if i & 128 else 1.0) * ((1.0 + (i & 7) / 8.0) * 2.0 ** (((i >> 3) & 15) - 7) if i & 120 else (i & 7) * 2.0 ** -9) for i in range(256)])


def e4m3fn_bytes(y):
    return np.clip(np.asarray(y, np.float64), -448.0, 448.0).astype(np.float32).astype(ml_dtypes.float8_e4m3fn).view(np.uint8)


def e4m3fn_values(b):
    return E4M3FN[b]


Q, D, C, P = 1024, 512, 128, 4096


def sigmoid(v):
    return 1.0 / (1.0 + np.exp(-v))


def object_class_probs(z, u):
    mx = np.maximum(np.max(z, axis=1), u)
    e = np.exp(z - mx[:, None])
    e_void = np.exp(u - mx)
    denom = np.sum(e, axis=1) + e_void
    return e / denom[:, None]


def draw0():
    a, b = mx_kscale(D), mx_kscale(D)
    t = mx_kscale(Q)
    sc = 2.0 / np.sqrt(D)
    emb = bf(np.random.standard_normal((Q, D)) * sc * a)
    pix = bf(np.random.standard_normal((P, D)) / a)
    queries = bf(np.random.standard_normal((Q, D)) * b)
    w_cls_words, w_cls_scales = pack_weight(np.random.standard_normal((D, C)) * sc / b[:, None], "e4m3")
    return {
        "emb": emb,
        "pix": pix,
        "queries": queries,
        "w_cls_words": w_cls_words,
        "w_cls_scales": w_cls_scales,
        "w_void": bf(np.random.standard_normal(D) * sc / b),
        "g_mask": bf((1.0 + 0.1 * np.random.standard_normal(Q)) / t),
        "g_cls": bf((1.0 + 0.1 * np.random.standard_normal(Q)) * t),
    }


def core(emb, pix, queries, w_cls_words, w_cls_scales, w_void, g_mask, g_cls):
    l = mxq(f64(emb), 1, "e4m3") @ mxq(f64(pix).T, 0, "e4m3")
    m = (sigmoid(l) - 0.5) * f64(g_mask)[:, None]
    z = mxq(f64(queries), 1, "e4m3") @ unpack_weight(w_cls_words, w_cls_scales, "e4m3")
    u = 6.0 + np.sum(f64(queries) * f64(w_void)[None, :], axis=1)
    prob = object_class_probs(z, u)
    s = (prob - np.mean(prob, axis=1, keepdims=True)) * f64(g_cls)[:, None]
    return mxq(s.T, 1, "e4m3") @ mxq(m, 0, "e4m3")


def setup_inputs():
    drawn = draw0()
    full = np.asarray(drawn['pix']).astype(np.float64)
    scale = (np.abs(full).reshape(4096, 4, 128).max(axis=(2,)) / 448.0).astype(np.float32)
    given = {}
    for key, value in drawn.items():
        if key == 'pix':
            given['pix_bytes'] = e4m3fn_bytes(full / np.repeat(scale.astype(np.float64), 128, axis=1))
            given['pix_scale'] = scale
        else:
            given[key] = value
    return given


def reference(emb, pix_bytes, pix_scale, queries, w_cls_words, w_cls_scales, w_void, g_mask, g_cls):
    return core(emb, e4m3fn_values(pix_bytes) * np.repeat(pix_scale.astype(np.float64), 128, axis=1), queries, w_cls_words, w_cls_scales, w_void, g_mask, g_cls)

@@ -1,0 +1,518 @@
+from contextlib import ExitStack
+
+import concourse.mybir as mybir
+from concourse.masks import make_identity
+
+Q, D, C, NPIX = 1024, 512, 128, 4096
+FLOPS = 2 * Q * D * NPIX + 2 * Q * D * C + 2 * C * Q * NPIX
+
+P = 128
+F32 = mybir.dt.float32
+BF16 = mybir.dt.bfloat16
+I32 = mybir.dt.int32
+U32 = mybir.dt.uint32
+U8 = mybir.dt.uint8
+FP8 = mybir.dt.float8_e4m3fn
+FP8X4 = mybir.dt.float8_e4m3fn_x4
+ACT = mybir.ActivationFunctionType
+ALU = mybir.AluOpType
+AX = mybir.AxisListType
+
+CHUNK = 512
+NCHUNK = NPIX // CHUNK
+NG = Q // 512
+NUNIT = NCHUNK * NG
+NS1 = 5
+NS2 = 1
+NS = (0,) * 16
+QENG = ("s", "s")
+QT = 2
+VQ = 3
+US = 2
+ZS = 4
+VM = 6
+XS = 8
+VS = 9
+OS = 13
+OD = 3
+OENG = "s"
+ALT = (2, 3, 4, 5)
+WL = 8
+WE = 8
+QL = 4
+QE = 2
+TL = 6
+KS = 6
+TB = 6
+MB = 12
+
+
+def tile_maskquerysemanticinference_d1p_kernel(
+    tc, emb, pix_bytes, pix_scale, queries, w_words, w_scales, w_void, g_mask, g_cls, out
+):
+    nc = tc.nc
+    with ExitStack() as ctx:
+        const = ctx.enter_context(tc.tile_pool(name="const", bufs=1))
+        work = ctx.enter_context(tc.tile_pool(name="work", bufs=1))
+        psum = ctx.enter_context(tc.psum_pool(name="psum", bufs=1))
+
+        ident = const.tile([P, P], F32, name="ident")
+        make_identity(nc, ident[:])
+        ctx.enter_context(tc.manual_schedule())
+
+        warm = const.tile([P, 1], F32, name="warm")
+        nc.vector.memset(warm[:], 0.0)
+        warm_out = const.tile([P, 1], F32, name="warm_out")
+        nc.scalar.activation(out=warm_out[:], in_=warm[:], func=ACT.Exp)
+
+        pixb = [const.tile([P, 4 * 512], U8, name="pixb%d" % c, align_bytes=64) for c in range(NCHUNK)]
+        pix_view = pix_bytes.rearrange("(c h p r) k -> c p h (r k)", h=2, p=P, r=2)
+        psc = const.tile([P, 2 * NCHUNK, 8], F32, name="psc")
+        psc_view = pix_scale.rearrange("(c p r) j -> p c (r j)", p=P, r=2)
+        emb_raw = [const.tile([P, 4, 512], BF16, name="emb_raw%d" % g, align_bytes=64) for g in range(NG)]
+        emb_view = emb.rearrange("(g p t) k -> g p t k", p=P, t=4)
+        q_raw = [const.tile([P, 4, 512], BF16, name="q_raw%d" % g, align_bytes=64) for g in range(NG)]
+        q_view = queries.rearrange("(g p t) k -> g p t k", p=P, t=4)
+
+        def load_pix(c, h):
+            nc.sync.dma_start(out=pixb[c][:, 1024 * h : 1024 * (h + 1)], in_=pix_view[c][:, h, :])
+
+        def load_rows(tile, view, h):
+            nc.sync.dma_start(out=tile[:, 2 * h : 2 * h + 2, :], in_=view[:, 2 * h : 2 * h + 2, :])
+
+        nc.sync.dma_start(out=psc[:, 0:2, :], in_=psc_view[:, 0:2, :])
+        load_pix(0, 0)
+        load_rows(emb_raw[0], emb_view[0], 0)
+        load_rows(emb_raw[0], emb_view[0], 1)
+        load_pix(0, 1)
+        nc.sync.dma_start(out=psc[:, 2:, :], in_=psc_view[:, 2:, :])
+        gm_b = const.tile([P, 8], BF16, name="gm_b")
+        nc.sync.dma_start(out=gm_b[:].rearrange("p (g t) -> p g t", t=4), in_=g_mask.rearrange("(g p t) -> p g t", p=P, t=4))
+        load_rows(emb_raw[1], emb_view[1], 0)
+        load_rows(emb_raw[1], emb_view[1], 1)
+        load_pix(1, 0)
+        load_pix(1, 1)
+        nc.sync.dma_start(out=pixb[2][:].rearrange("p (h x) -> p h x", h=2), in_=pix_view[2])
+        for g in range(NG):
+            nc.sync.dma_start(out=q_raw[g][:], in_=q_view[g])
+        w_sc = const.tile([P, C], U8, name="w_sc", align_bytes=64)
+        nc.vector.memset(w_sc[:].bitcast(I32), 0)
+        for r in range(4):
+            nc.sync.dma_start(
+                out=w_sc[32 * r : 32 * r + 4, :].bitcast(I32), in_=w_scales[0, 4 * r : 4 * r + 4, :].bitcast(I32)
+            )
+        w_codes = const.tile([P, 4 * C], U8, name="w_codes", align_bytes=64)
+        nc.sync.dma_start(out=w_codes[:].bitcast(I32), in_=w_words[0].rearrange("p n t -> p (n t)").bitcast(I32))
+        wv = const.tile([P, 4], BF16, name="wv")
+        nc.sync.dma_start(out=wv[:], in_=w_void.rearrange("(p t) -> p t", t=4))
+        gc_b = const.tile([P, 8], BF16, name="gc_b")
+        nc.sync.dma_start(out=gc_b[:].rearrange("p (g t) -> p g t", t=4), in_=g_cls.rearrange("(g p t) -> p g t", p=P, t=4))
+        for c in range(3, NCHUNK):
+            nc.sync.dma_start(out=pixb[c][:].rearrange("p (h x) -> p h x", h=2), in_=pix_view[c])
+
+        ident_b = const.tile([P, P], BF16, name="ident_b")
+        g2b = const.tile([P, 8], BF16, name="g2b")
+        g2s = const.tile([P, 8], F32, name="g2s")
+        g2p = psum.tile([P, 512], F32, name="g2p", tag="g2p", bufs=1)
+
+        wides = {}
+        pgroup = {}
+        pcodes = {}
+        psts = {}
+
+        def widen(c, r, j, eng):
+            if c not in wides:
+                wides[c] = work.tile([P, 4, 512], BF16, name="wide", tag="wide", bufs=6, align_bytes=64)
+            src = pixb[c][:, 512 * r + 128 * j : 512 * r + 128 * (j + 1)].bitcast(FP8)
+            dst = wides[c][:, r, 128 * j : 128 * (j + 1)]
+            scl = psc[:, 2 * c + r // 2, 4 * (r % 2) + j : 4 * (r % 2) + j + 1]
+            if eng == "v":
+                nc.vector.tensor_scalar(out=dst, in0=src, scalar1=scl, scalar2=None, op0=ALU.mult)
+            else:
+                nc.scalar.activation(out=dst, in_=src, func=ACT.Copy, scale=scl)
+
+        def transposes(rows, h, tag, bufs):
+            bank = psum.tile([P, 512], F32, name="bank_" + tag, tag=tag, bufs=bufs)
+            b4 = bank[:].rearrange("p (s u m) -> p s u m", s=2, u=2)
+            for s in range(2):
+                words = rows[:, 2 * h + s, :].bitcast(F32)
+                for u in range(2):
+                    nc.tensor.transpose(b4[:, s, u, :], words[:, u::2], ident[:])
+            return b4
+
+        def bank_copy(eng, dst, src):
+            if eng == "v":
+                nc.vector.tensor_copy(out=dst, in_=src)
+            else:
+                nc.scalar.copy(out=dst, in_=src)
+
+        def stat_group(name):
+            return work.tile([P, 2048], BF16, name=name, tag="sgroup", bufs=4, align_bytes=64)
+
+        def stat_copy(eng, grp, h, b4):
+            dst = grp[:].bitcast(F32).rearrange("p (s m u) -> p s m u", s=4, u=2)[:, 2 * h : 2 * h + 2]
+            bank_copy(eng, dst, b4.rearrange("p s u m -> p s m u"))
+
+        def pix_copy(eng, c, h, b4):
+            if c not in pgroup:
+                pgroup[c] = work.tile([P, 2048], BF16, name="pgroup", tag="pgroup", bufs=5, align_bytes=64)
+            dst = pgroup[c][:].bitcast(F32)[:, 512 * h : 512 * (h + 1)].rearrange("p (m s u) -> p m s u", s=2, u=2)
+            bank_copy(eng, dst, b4.rearrange("p s u m -> p m s u"))
+
+        def quant(codes, scales, grp):
+            nc.vector.quantize_mx(out=codes.bitcast(FP8X4), scales=scales, in_=grp)
+
+        def pix_quant(c, n0, n1):
+            if c not in pcodes:
+                pcodes[c] = work.tile([P, 512], U32, name="pcodes", tag="pcodes", bufs=6, align_bytes=64)
+                psts[c] = work.tile([P, 512], U8, name="psts", tag="psts", bufs=6, align_bytes=64)
+            quant(pcodes[c][:, n0:n1], psts[c][:, n0:n1], pgroup[c][:, 4 * n0 : 4 * n1])
+
+        def mm(o, lc, ls, rc, rs, start=True, stop=True):
+            nc.tensor.matmul_mx(
+                out=o, lhsT=lc.bitcast(FP8X4), lhsT_scale=ls, rhs=rc.bitcast(FP8X4), rhs_scale=rs, start=start, stop=stop
+            )
+
+        ecodes = [const.tile([P, 512], U32, name="ecodes%d" % g, align_bytes=64) for g in range(NG)]
+        escales = [const.tile([P, 512], U8, name="escales%d" % g, align_bytes=64) for g in range(NG)]
+        qcodes = [const.tile([P, 512], U32, name="qcodes%d" % g, align_bytes=64) for g in range(NG)]
+        qscales = [const.tile([P, 512], U8, name="qscales%d" % g, align_bytes=64) for g in range(NG)]
+        scodes = [const.tile([P, C], U32, name="scodes%d" % g, align_bytes=64) for g in range(NG)]
+        sscales = [const.tile([P, C], U8, name="sscales%d" % g, align_bytes=64) for g in range(NG)]
+
+        lbank = {}
+        tanh_t = {}
+        mcodes = {}
+        mscales = {}
+        mtile = {}
+
+        def logits(i, j):
+            c, g = divmod(i, NG)
+            bank = psum.tile([P, 512], F32, name="lbank", tag="l", bufs=3)
+            for t in range(4):
+                mm(
+                    bank[:, 128 * t : 128 * (t + 1)],
+                    ecodes[g][:, 128 * t : 128 * (t + 1)],
+                    escales[g][:, 128 * t : 128 * (t + 1)],
+                    pcodes[c][:, 128 * j : 128 * (j + 1)],
+                    psts[c][:, 128 * j : 128 * (j + 1)],
+                )
+            lbank[i, j] = bank
+
+        def tanh(i, j):
+            if i not in tanh_t:
+                tanh_t[i] = work.tile([P, 512, 4], F32, name="tanh", tag="tanh", bufs=TB, align_bytes=64)
+            nc.scalar.activation(
+                out=tanh_t[i][:, 128 * j : 128 * (j + 1), :],
+                in_=lbank[i, j][:].rearrange("p (t n) -> p n t", t=4),
+                func=ACT.Tanh,
+                scale=0.5,
+            )
+
+        def gain(i, n0, n1):
+            g = i % NG
+            if i not in mtile:
+                mtile[i] = work.tile([P, 512, 4], BF16, name="mtile", tag="mtile", bufs=3, align_bytes=64)
+            nc.vector.tensor_tensor(
+                out=mtile[i][:, n0:n1, :],
+                in0=tanh_t[i][:, n0:n1, :],
+                in1=g2p[:, 4 * g : 4 * g + 4].unsqueeze(1).broadcast_to([P, n1 - n0, 4]),
+                op=ALU.mult,
+            )
+
+        def gain_g(i):
+            g = i % NG
+            mtile[i] = work.tile([P, 512, 4], BF16, name="mtile_g", tag="mtile_g", bufs=1, align_bytes=64)
+            nc.gpsimd.tensor_tensor(
+                out=mtile[i][:],
+                in0=tanh_t[i][:],
+                in1=g2s[:, 4 * g : 4 * g + 4].unsqueeze(1).broadcast_to([P, 512, 4]),
+                op=ALU.mult,
+            )
+
+        def m_quant(i, n0, n1):
+            if i not in mcodes:
+                mcodes[i] = work.tile([P, 512], U32, name="mcodes", tag="mcodes", bufs=MB, align_bytes=64)
+                mscales[i] = work.tile([P, 512], U8, name="mscales", tag="mscales", bufs=MB, align_bytes=64)
+            quant(
+                mcodes[i][:, n0:n1], mscales[i][:, n0:n1], mtile[i][:, n0:n1, :].rearrange("p n t -> p (n t)")
+            )
+
+        obank = {}
+
+        def out_mm(c, n0, n1):
+            if c not in obank:
+                obank[c] = psum.tile([P, 512], F32, name="obank", tag="o", bufs=3)
+            for g in range(NG):
+                i = NG * c + g
+                mm(
+                    obank[c][:, n0:n1], scodes[g][:], sscales[g][:], mcodes[i][:, n0:n1], mscales[i][:, n0:n1],
+                    start=(g == 0), stop=(g == NG - 1),
+                )
+
+        osb = {}
+
+        def out_copy(eng, c, n0, n1):
+            if c not in osb:
+                osb[c] = work.tile([P, 512], F32, name="osb", tag="osb", bufs=3)
+            bank_copy(eng, osb[c][:, n0:n1], obank[c][:, n0:n1])
+
+        def store(c, n0, n1):
+            nc.sync.dma_start(out=out[:, 512 * c + n0 : 512 * c + n1], in_=osb[c][:, n0:n1])
+
+        def widen_half(c, h, n_s):
+            for b in range(8):
+                r, j = 2 * h + b // 4, b % 4
+                widen(c, r, j, "s" if b >= 8 - n_s else "v")
+
+        def widen_v(k, n_s):
+            c, h = divmod(k, 2)
+            for b in range(8 - n_s):
+                widen(c, 2 * h + b // 4, b % 4, "v")
+
+        def widen_s(k, n_s):
+            c, h = divmod(k, 2)
+            for b in range(8 - n_s, 8):
+                widen(c, 2 * h + b // 4, b % 4, "s")
+
+        prep_bank = {}
+
+        def prep_t(k):
+            tag, bufs = ("tr", 1) if k not in ALT else ("o", 3)
+            prep_bank[k] = transposes(wides[k // 2], k % 2, tag, bufs)
+
+        def prep_copy(k, eng):
+            pix_copy(eng, k // 2, k % 2, prep_bank[k])
+
+        def prep_q(k):
+            pix_quant(k // 2, 256 * (k % 2), 256 * (k % 2 + 1))
+
+        zb = [None, None]
+        um = const.tile([P, 8], F32, name="um")
+        zmx = const.tile([P, 8], F32, name="zmx")
+        nmx = const.tile([P, 8], F32, name="nmx")
+        esum = const.tile([P, 8], F32, name="esum")
+        evoid = const.tile([P, 8], F32, name="evoid")
+        mean = const.tile([P, 8], F32, name="mean")
+        amp = const.tile([P, 8], F32, name="amp")
+        ez = const.tile([P, 8, C], F32, name="ez")
+        sgrp = [const.tile([P, C, 4], BF16, name="sgrp%d" % g, align_bytes=64) for g in range(NG)]
+        def class_logits(g):
+            zb[g] = psum.tile([P, 512], F32, name="zbank", tag="o", bufs=3)
+            for t in range(4):
+                mm(
+                    zb[g][:, 128 * t : 128 * (t + 1)],
+                    qcodes[g][:, 128 * t : 128 * (t + 1)],
+                    qscales[g][:, 128 * t : 128 * (t + 1)],
+                    w_codes[:].bitcast(U32),
+                    w_sc[:],
+                )
+
+        ubank = {}
+
+        def void_logits(cols):
+            if not ubank:
+                ubank[0] = psum.tile([P, 512], F32, name="ubank", tag="o", bufs=3)
+            for col in cols:
+                q4 = qg[col // 4][:].rearrange("p (s m k) -> p s m k", s=4, k=4)
+                for k in range(4):
+                    nc.tensor.matmul(
+                        ubank[0][:, col : col + 1], q4[:, col % 4, :, k], wv[:, k : k + 1], start=(k == 0), stop=(k == 3)
+                    )
+
+        def void_read():
+            nc.vector.tensor_scalar(out=um[:], in0=ubank[0][:, 0:8], scalar1=6.0, scalar2=None, op0=ALU.add)
+
+        def class_max(g):
+            nc.vector.tensor_reduce(
+                out=zmx[:, 4 * g : 4 * g + 4],
+                in_=zb[g][:].rearrange("p (t c) -> p t c", t=4),
+                axis=AX.X,
+                op=ALU.max,
+            )
+
+        def class_shift():
+            nc.vector.tensor_tensor(out=zmx[:], in0=zmx[:], in1=um[:], op=ALU.max)
+            nc.vector.tensor_scalar(out=nmx[:], in0=zmx[:], scalar1=-1.0, scalar2=None, op0=ALU.mult)
+            nc.vector.tensor_tensor(out=um[:], in0=um[:], in1=zmx[:], op=ALU.subtract)
+
+        def class_exp(ks):
+            for k in ks:
+                nc.scalar.activation(
+                    out=ez[:, k, :],
+                    in_=zb[k // 4][:, 128 * (k % 4) : 128 * (k % 4 + 1)],
+                    func=ACT.Exp,
+                    bias=nmx[:, k : k + 1],
+                    scale=1.0,
+                    accum_out=esum[:, k : k + 1],
+                )
+
+        def class_factors():
+            nc.vector.tensor_tensor(out=evoid[:], in0=evoid[:], in1=esum[:], op=ALU.add)
+            nc.vector.tensor_scalar(out=mean[:], in0=esum[:], scalar1=1.0 / C, scalar2=None, op0=ALU.mult)
+            nc.vector.reciprocal(out=evoid[:], in_=evoid[:])
+            nc.vector.tensor_tensor(out=amp[:], in0=evoid[:], in1=gc_b[:], op=ALU.mult)
+
+        def class_scores():
+            for k in range(8):
+                nc.vector.tensor_scalar(
+                    out=sgrp[k // 4][:, :, k % 4],
+                    in0=ez[:, k, :],
+                    scalar1=mean[:, k : k + 1],
+                    scalar2=amp[:, k : k + 1],
+                    op0=ALU.subtract,
+                    op1=ALU.mult,
+                )
+            for g in range(NG):
+                quant(scodes[g][:], sscales[g][:], sgrp[g][:].rearrange("p c t -> p (c t)"))
+
+        eg = [stat_group("eg0"), stat_group("eg1")]
+        qg = [None, None]
+        nc.vector.tensor_copy(out=ident_b[:], in_=ident[:])
+        widen_v(0, 4)
+        widen_s(0, 4)
+        prep_t(0)
+        ea = transposes(emb_raw[0], 0, "o", 3)
+        eb = transposes(emb_raw[0], 1, "o", 3)
+        prep_copy(0, "s")
+        stat_copy("v", eg[0], 0, ea)
+        stat_copy("s", eg[0], 1, eb)
+        prep_q(0)
+        quant(ecodes[0][:, 0:256], escales[0][:, 0:256], eg[0][:, 0:1024])
+        quant(ecodes[0][:, 256:512], escales[0][:, 256:512], eg[0][:, 1024:2048])
+        logits(0, 0)
+        logits(0, 1)
+        widen_v(1, NS1)
+        widen_s(1, NS1)
+        prep_t(1)
+        e1a = transposes(emb_raw[1], 0, "o", 3)
+        e1b = transposes(emb_raw[1], 1, "o", 3)
+        prep_copy(1, "v")
+        prep_q(1)
+        tanh(0, 0)
+        tanh(0, 1)
+        logits(0, 2)
+        logits(0, 3)
+        stat_copy("s", eg[1], 0, e1a)
+        stat_copy("s", eg[1], 1, e1b)
+        tanh(0, 2)
+        tanh(0, 3)
+        quant(ecodes[1][:], escales[1][:], eg[1][:])
+        for k in (2, 3):
+            widen_v(k, NS2)
+            widen_s(k, NS2)
+        for k in (2, 3):
+            prep_t(k)
+        for k in (2, 3):
+            prep_copy(k, "v")
+        for k in (2, 3):
+            prep_q(k)
+        nc.vector.tensor_scalar(out=g2b[:], in0=gm_b[:], scalar1=0.5, scalar2=None, op0=ALU.mult)
+        nc.tensor.matmul(g2p[:, 0:8], ident_b[:], g2b[:], start=True, stop=True)
+
+        next_out = 0
+        pending = []
+        NK = 2 * NCHUNK
+        ks = range(4, NK)
+        w_at = {}
+        q_at = {}
+        t_at = {}
+        for k in ks:
+            w_at.setdefault(max(1, 3 * ((k - WL) // 3)) if k >= WE else 1, []).append(k)
+            q_at.setdefault(max(QE, 3 * ((k - QL) // 3)), []).append(k)
+            t_at.setdefault(max(1 + (k - 4) // 3, k - TL), []).append(k)
+
+        for i in range(1, NUNIT + 1):
+            live = i < NUNIT
+            group = i % 3 == 0
+            ts = t_at.get(i, [])
+            if live:
+                logits(i, 0)
+                logits(i, 1)
+                tanh(i, 0)
+                tanh(i, 1)
+            if group:
+                if i == 3:
+                    nc.vector.tensor_scalar(out=g2s[:], in0=gm_b[:], scalar1=0.5, scalar2=None, op0=ALU.mult)
+                gain_g(i - 3)
+                gain(i - 2, 0, 512)
+                gain(i - 1, 0, 512)
+            if i == VM:
+                void_read()
+                class_max(0)
+                class_max(1)
+            if i == VM:
+                class_shift()
+            if i == VS:
+                class_factors()
+            for k in w_at.get(i, []):
+                widen_v(k, NS[k])
+                widen_s(k, NS[k])
+            for k in ts:
+                prep_t(k)
+                prep_copy(k, "s" if k >= KS else "v")
+            if i in (QT, QT + 1):
+                g = i - QT
+                qg[g] = stat_group("qg%d" % g)
+                qa = [transposes(q_raw[g], h, "o", 3) for h in range(2)]
+            if live:
+                logits(i, 2)
+                logits(i, 3)
+            if i in (QT, QT + 1):
+                for h in range(2):
+                    stat_copy(QENG[h], qg[g], h, qa[h])
+            if live:
+                tanh(i, 2)
+                tanh(i, 3)
+            for c in pending:
+                out_copy(OENG, c, 0, 512)
+                store(c, 0, 512)
+            pending = []
+            if i == VQ:
+                for g in range(NG):
+                    quant(qcodes[g][:], qscales[g][:], qg[g][:])
+            if i == VS:
+                class_scores()
+            if group:
+                m_quant(i - 2, 0, 512)
+                m_quant(i - 1, 0, 512)
+            for k in q_at.get(i, []):
+                prep_q(k)
+            if group:
+                m_quant(i - 3, 0, 512)
+            if US <= i < US + 4:
+                void_logits((2 * (i - US), 2 * (i - US) + 1))
+            if i in (ZS, ZS + 1):
+                class_logits(i - ZS)
+            if i == XS:
+                class_exp(range(8))
+                nc.scalar.activation(out=evoid[:], in_=um[:], func=ACT.Exp)
+            if i >= OS:
+                ready = 3 * ((i - OD) // 3) - 1
+                while next_out < NCHUNK - 1 and NG * next_out + 1 <= ready and len(pending) < 2:
+                    out_mm(next_out, 0, 512)
+                    pending.append(next_out)
+                    next_out += 1
+            if i == NUNIT:
+                while pending or next_out < NCHUNK - 1:
+                    for c in pending:
+                        out_copy("s", c, 0, 512)
+                        store(c, 0, 512)
+                    pending = []
+                    while next_out < NCHUNK - 1 and len(pending) < 2:
+                        out_mm(next_out, 0, 512)
+                        pending.append(next_out)
+                        next_out += 1
+                last = NUNIT - 1
+                for b in range(4):
+                    gain(last, 128 * b, 128 * (b + 1))
+                    if b > 0:
+                        m_quant(last, 128 * (b - 1), 128 * b)
+                        out_mm(NCHUNK - 1, 128 * (b - 1), 128 * b)
+                        out_copy("s", NCHUNK - 1, 128 * (b - 1), 128 * b)
+                    if b == 2:
+                        store(NCHUNK - 1, 0, 256)
+                m_quant(last, 384, 512)
+                out_mm(NCHUNK - 1, 384, 512)
+                out_copy("s", NCHUNK - 1, 384, 512)
+                store(NCHUNK - 1, 256, 512)

@@ -22,29 +22,30 @@ CHUNK = 512
 NCHUNK = NPIX // CHUNK
 NG = Q // 512
 NUNIT = NCHUNK * NG
-NS1 = 5
-NS2 = 1
-NS = (0,) * 16
-QENG = ("s", "s")
-QT = 2
-VQ = 3
-US = 2
-ZS = 4
-VM = 6
-XS = 8
-VS = 9
-OS = 13
-OD = 3
-OENG = "s"
+NS1 = 4
+NS2 = 0
+NS = (2,) * 10 + (0,) * 6
+EARLYW = 1
+C2 = "v"
+C3 = "v"
+WLAST = 11
+WL = 10
+QL = 3
+TL = 4
+TR = 3
+WS = 8
+VM = 2
+VQ = 1
+QT = 4
+US = 5
+UN = 2
+ZS = 7
+XS = 11
+OUTS = {13: 1, 14: 1}
+OCS = {14: 2}
 ALT = (2, 3, 4, 5)
-WL = 8
-WE = 8
-QL = 4
-QE = 2
-TL = 6
-KS = 6
-TB = 6
-MB = 12
+TB = 5
+MB = 15
 
 
 def tile_maskquerysemanticinference_d1p_kernel(
@@ -122,7 +123,7 @@ def tile_maskquerysemanticinference_d1p_kernel(
 
         def widen(c, r, j, eng):
             if c not in wides:
-                wides[c] = work.tile([P, 4, 512], BF16, name="wide", tag="wide", bufs=6, align_bytes=64)
+                wides[c] = work.tile([P, 4, 512], BF16, name="wide", tag="wide", bufs=5, align_bytes=64)
             src = pixb[c][:, 512 * r + 128 * j : 512 * r + 128 * (j + 1)].bitcast(FP8)
             dst = wides[c][:, r, 128 * j : 128 * (j + 1)]
             scl = psc[:, 2 * c + r // 2, 4 * (r % 2) + j : 4 * (r % 2) + j + 1]
@@ -147,7 +148,7 @@ def tile_maskquerysemanticinference_d1p_kernel(
                 nc.scalar.copy(out=dst, in_=src)
 
         def stat_group(name):
-            return work.tile([P, 2048], BF16, name=name, tag="sgroup", bufs=4, align_bytes=64)
+            return work.tile([P, 2048], BF16, name=name, tag="sgroup", bufs=3, align_bytes=64)
 
         def stat_copy(eng, grp, h, b4):
             dst = grp[:].bitcast(F32).rearrange("p (s m u) -> p s m u", s=4, u=2)[:, 2 * h : 2 * h + 2]
@@ -155,7 +156,7 @@ def tile_maskquerysemanticinference_d1p_kernel(
 
         def pix_copy(eng, c, h, b4):
             if c not in pgroup:
-                pgroup[c] = work.tile([P, 2048], BF16, name="pgroup", tag="pgroup", bufs=5, align_bytes=64)
+                pgroup[c] = work.tile([P, 2048], BF16, name="pgroup", tag="pgroup", bufs=4, align_bytes=64)
             dst = pgroup[c][:].bitcast(F32)[:, 512 * h : 512 * (h + 1)].rearrange("p (m s u) -> p m s u", s=2, u=2)
             bank_copy(eng, dst, b4.rearrange("p s u m -> p m s u"))
 
@@ -164,8 +165,8 @@ def tile_maskquerysemanticinference_d1p_kernel(
 
         def pix_quant(c, n0, n1):
             if c not in pcodes:
-                pcodes[c] = work.tile([P, 512], U32, name="pcodes", tag="pcodes", bufs=6, align_bytes=64)
-                psts[c] = work.tile([P, 512], U8, name="psts", tag="psts", bufs=6, align_bytes=64)
+                pcodes[c] = work.tile([P, 512], U32, name="pcodes", tag="pcodes", bufs=5, align_bytes=64)
+                psts[c] = work.tile([P, 512], U8, name="psts", tag="psts", bufs=5, align_bytes=64)
             quant(pcodes[c][:, n0:n1], psts[c][:, n0:n1], pgroup[c][:, 4 * n0 : 4 * n1])
 
         def mm(o, lc, ls, rc, rs, start=True, stop=True):
@@ -254,7 +255,7 @@ def tile_maskquerysemanticinference_d1p_kernel(
 
         def out_copy(eng, c, n0, n1):
             if c not in osb:
-                osb[c] = work.tile([P, 512], F32, name="osb", tag="osb", bufs=3)
+                osb[c] = work.tile([P, 512], F32, name="osb", tag="osb", bufs=6)
             bank_copy(eng, osb[c][:, n0:n1], obank[c][:, n0:n1])
 
         def store(c, n0, n1):
@@ -265,6 +266,7 @@ def tile_maskquerysemanticinference_d1p_kernel(
                 r, j = 2 * h + b // 4, b % 4
                 widen(c, r, j, "s" if b >= 8 - n_s else "v")
 
+        qg = [None, None]
         def widen_v(k, n_s):
             c, h = divmod(k, 2)
             for b in range(8 - n_s):
@@ -366,153 +368,250 @@ def tile_maskquerysemanticinference_d1p_kernel(
             for g in range(NG):
                 quant(scodes[g][:], sscales[g][:], sgrp[g][:].rearrange("p c t -> p (c t)"))
 
+
+        queue = {"t": [], "s": [], "v": [], "g": []}
+
+        def put(eng, makes, needs, fn, *args):
+            queue[eng].append((makes, needs, fn, args))
+
         eg = [stat_group("eg0"), stat_group("eg1")]
-        qg = [None, None]
-        nc.vector.tensor_copy(out=ident_b[:], in_=ident[:])
-        widen_v(0, 4)
-        widen_s(0, 4)
-        prep_t(0)
-        ea = transposes(emb_raw[0], 0, "o", 3)
-        eb = transposes(emb_raw[0], 1, "o", 3)
-        prep_copy(0, "s")
-        stat_copy("v", eg[0], 0, ea)
-        stat_copy("s", eg[0], 1, eb)
-        prep_q(0)
-        quant(ecodes[0][:, 0:256], escales[0][:, 0:256], eg[0][:, 0:1024])
-        quant(ecodes[0][:, 256:512], escales[0][:, 256:512], eg[0][:, 1024:2048])
-        logits(0, 0)
-        logits(0, 1)
-        widen_v(1, NS1)
-        widen_s(1, NS1)
-        prep_t(1)
-        e1a = transposes(emb_raw[1], 0, "o", 3)
-        e1b = transposes(emb_raw[1], 1, "o", 3)
-        prep_copy(1, "v")
-        prep_q(1)
-        tanh(0, 0)
-        tanh(0, 1)
-        logits(0, 2)
-        logits(0, 3)
-        stat_copy("s", eg[1], 0, e1a)
-        stat_copy("s", eg[1], 1, e1b)
-        tanh(0, 2)
-        tanh(0, 3)
-        quant(ecodes[1][:], escales[1][:], eg[1][:])
-        for k in (2, 3):
-            widen_v(k, NS2)
-            widen_s(k, NS2)
-        for k in (2, 3):
-            prep_t(k)
-        for k in (2, 3):
-            prep_copy(k, "v")
-        for k in (2, 3):
-            prep_q(k)
-        nc.vector.tensor_scalar(out=g2b[:], in0=gm_b[:], scalar1=0.5, scalar2=None, op0=ALU.mult)
-        nc.tensor.matmul(g2p[:, 0:8], ident_b[:], g2b[:], start=True, stop=True)
+        ebank = {}
 
-        next_out = 0
-        pending = []
-        NK = 2 * NCHUNK
-        ks = range(4, NK)
-        w_at = {}
-        q_at = {}
-        t_at = {}
-        for k in ks:
-            w_at.setdefault(max(1, 3 * ((k - WL) // 3)) if k >= WE else 1, []).append(k)
-            q_at.setdefault(max(QE, 3 * ((k - QL) // 3)), []).append(k)
-            t_at.setdefault(max(1 + (k - 4) // 3, k - TL), []).append(k)
+        def et(g, h):
+            ebank[g, h] = transposes(emb_raw[g], h, "o", 3)
 
-        for i in range(1, NUNIT + 1):
-            live = i < NUNIT
-            group = i % 3 == 0
-            ts = t_at.get(i, [])
-            if live:
-                logits(i, 0)
-                logits(i, 1)
-                tanh(i, 0)
-                tanh(i, 1)
-            if group:
-                if i == 3:
-                    nc.vector.tensor_scalar(out=g2s[:], in0=gm_b[:], scalar1=0.5, scalar2=None, op0=ALU.mult)
-                gain_g(i - 3)
-                gain(i - 2, 0, 512)
-                gain(i - 1, 0, 512)
-            if i == VM:
-                void_read()
-                class_max(0)
-                class_max(1)
-            if i == VM:
-                class_shift()
-            if i == VS:
-                class_factors()
-            for k in w_at.get(i, []):
-                widen_v(k, NS[k])
-                widen_s(k, NS[k])
-            for k in ts:
-                prep_t(k)
-                prep_copy(k, "s" if k >= KS else "v")
-            if i in (QT, QT + 1):
-                g = i - QT
+        def ecp(eng, g, h):
+            stat_copy(eng, eg[g], h, ebank[g, h])
+
+        def eq(g, h):
+            quant(ecodes[g][:, 256 * h : 256 * h + 256], escales[g][:, 256 * h : 256 * h + 256], eg[g][:, 1024 * h : 1024 * h + 1024])
+
+        def qt(g, h):
+            if h == 0:
                 qg[g] = stat_group("qg%d" % g)
-                qa = [transposes(q_raw[g], h, "o", 3) for h in range(2)]
-            if live:
-                logits(i, 2)
-                logits(i, 3)
-            if i in (QT, QT + 1):
-                for h in range(2):
-                    stat_copy(QENG[h], qg[g], h, qa[h])
-            if live:
-                tanh(i, 2)
-                tanh(i, 3)
-            for c in pending:
-                out_copy(OENG, c, 0, 512)
-                store(c, 0, 512)
-            pending = []
-            if i == VQ:
+            ebank[g + 2, h] = transposes(q_raw[g], h, "o", 3)
+
+        def qcp(eng, g, h):
+            stat_copy(eng, qg[g], h, ebank[g + 2, h])
+
+        def qq(g):
+            quant(qcodes[g][:], qscales[g][:], qg[g][:])
+
+        def g2_make():
+            nc.vector.tensor_scalar(out=g2b[:], in0=gm_b[:], scalar1=0.5, scalar2=None, op0=ALU.mult)
+
+        def g2_bank():
+            nc.tensor.matmul(g2p[:, 0:8], ident_b[:], g2b[:], start=True, stop=True)
+
+        def g2_sbuf():
+            nc.vector.tensor_scalar(out=g2s[:], in0=gm_b[:], scalar1=0.5, scalar2=None, op0=ALU.mult)
+
+        def exp_void():
+            nc.scalar.activation(out=evoid[:], in_=um[:], func=ACT.Exp)
+
+        def ident_copy():
+            nc.vector.tensor_copy(out=ident_b[:], in_=ident[:])
+
+        def put_w(k, n_s):
+            if n_s < 8:
+                put("v", ("wv", k), [], widen_v, k, n_s)
+            if n_s > 0:
+                put("s", ("ws", k), [], widen_s, k, n_s)
+
+        NK = 2 * NCHUNK
+        NSS = [4, NS1, NS2, NS2] + list(NS[4:])
+
+        def put_t(k):
+            put("t", ("t", k), ([("wv", k)] if NSS[k] < 8 else []) + ([("ws", k)] if NSS[k] > 0 else []), prep_t, k)
+
+        def put_c(k, eng):
+            put(eng, ("c", k), [("t", k)], prep_copy, k, eng)
+
+        def put_q(k):
+            put("v", ("q", k), [("c", k)], prep_q, k)
+
+        def put_l(i, j):
+            c, g = divmod(i, NG)
+            put("t", ("l", i, j), [("q", 2 * c + j // 2), ("eq", g, 0), ("eq", g, 1)], logits, i, j)
+
+        def put_h(i, j):
+            put("s", ("h", i, j), [("l", i, j)], tanh, i, j)
+
+        def put_gain(i):
+            put("v", ("m", i), [("h", i, j) for j in range(4)] + ["g2p"], gain, i, 0, 512)
+
+        def put_gain_g(i):
+            put("g", ("m", i), [("h", i, j) for j in range(4)] + ["g2s"], gain_g, i)
+
+        def put_mq(i):
+            put("v", ("mq", i), [("m", i)], m_quant, i, 0, 512)
+
+        def put_out(c):
+            put("t", ("o", c), ["sq", ("mq", 2 * c), ("mq", 2 * c + 1)], out_mm, c, 0, 512)
+
+        def put_oc(c, eng="s"):
+            put(eng, ("oc", c), [("o", c)], out_copy, eng, c, 0, 512)
+            put("y", ("st", c), [("oc", c)], store, c, 0, 512)
+
+        queue["y"] = []
+
+        put("v", "ident_b", [], ident_copy)
+        put_w(0, 4)
+        put("v", ("ec", 0, 0), [("et", 0, 0)], ecp, "v", 0, 0)
+        put_q(0)
+        put("v", ("eq", 0, 0), [("ec", 0, 0)], eq, 0, 0)
+        put("v", ("eq", 0, 1), [("ec", 0, 1)], eq, 0, 1)
+        put_c(0, "s")
+        put("s", ("ec", 0, 1), [("et", 0, 1)], ecp, "s", 0, 1)
+        put_w(1, NS1)
+        put("v", "g2b", [], g2_make)
+        if EARLYW:
+            put_w(2, NS2)
+        put_c(1, "v")
+        put_q(1)
+        put("s", ("ec", 1, 0), [("et", 1, 0)], ecp, "s", 1, 0)
+        put_h(0, 0)
+        put_h(0, 1)
+        put("s", ("ec", 1, 1), [("et", 1, 1)], ecp, "s", 1, 1)
+        put("v", ("eq", 1, 0), [("ec", 1, 0)], eq, 1, 0)
+        put("v", ("eq", 1, 1), [("ec", 1, 1)], eq, 1, 1)
+        if not EARLYW:
+            put_w(2, NS2)
+        put_w(3, NS2)
+        put_h(0, 2)
+        put_h(0, 3)
+        put_c(2, C2)
+        put_c(3, C3)
+        put_q(2)
+        put_q(3)
+        put_t(0)
+        for h in range(2):
+            put("t", ("et", 0, h), [], et, 0, h)
+        put_l(0, 0)
+        put_l(0, 1)
+        put_t(1)
+        for h in range(2):
+            put("t", ("et", 1, h), [], et, 1, h)
+        put_l(0, 2)
+        put_l(0, 3)
+        put_t(2)
+        put("t", "g2p", ["g2b", "ident_b"], g2_bank)
+        put_l(1, 0)
+        put_l(1, 1)
+        put_t(3)
+        put_h(1, 0)
+        put_h(1, 1)
+
+        wplan = {}
+        for k in range(4, NK):
+            wplan.setdefault(0 if k <= WLAST else max(1, (k - WL) // 3), []).append(k)
+        qplan = {}
+        for k in range(4, NK):
+            qplan.setdefault(max(0, (k - QL) // 3), []).append(k)
+        tplan = {}
+        for k in range(4, NK):
+            tplan.setdefault(max(1 + (k - 4) // TR, k - TL), []).append(k)
+
+        for k in wplan[0]:
+            put_w(k, NSS[k]) if NSS[k] == 0 else put("v", ("wv", k), [], widen_v, k, NSS[k])
+        for k in qplan.get(0, []):
+            put_q(k)
+        for grp in range(5):
+            a = 3 * grp
+            if grp == 0:
+                put("v", "g2s", [], g2_sbuf)
+            put_gain_g(a)
+            put_gain(a + 1)
+            put_gain(a + 2)
+            if grp == VM:
+                put("v", "um", [("u", n) for n in range(8)], void_read)
                 for g in range(NG):
-                    quant(qcodes[g][:], qscales[g][:], qg[g][:])
-            if i == VS:
-                class_scores()
-            if group:
-                m_quant(i - 2, 0, 512)
-                m_quant(i - 1, 0, 512)
-            for k in q_at.get(i, []):
-                prep_q(k)
-            if group:
-                m_quant(i - 3, 0, 512)
-            if US <= i < US + 4:
-                void_logits((2 * (i - US), 2 * (i - US) + 1))
+                    put("v", ("zm", g), [("z", g)], class_max, g)
+                put("v", "shift", ["um", ("zm", 0), ("zm", 1)], class_shift)
+            if grp == VM + 1:
+                put("v", "fac", [("x", k) for k in range(8)] + ["xv"], class_factors)
+            for k in wplan.get(grp + 1, []):
+                put("v", ("wv", k), [], widen_v, k, NSS[k])
+            if grp == VQ:
+                put("v", ("qq", 0), [("qc", 0, 0), ("qc", 0, 1)], qq, 0)
+                put("v", ("qq", 1), [("qc", 1, 0), ("qc", 1, 1)], qq, 1)
+            put_mq(a + 1)
+            put_mq(a + 2)
+            if grp == VM + 1:
+                put("v", "sq", ["fac"], class_scores)
+            for k in qplan.get(grp + 1, []):
+                put_q(k)
+            put_mq(a)
+        nout = 0
+        for i in range(1, NUNIT):
+            ts = tplan.get(i, [])
+            if i > 1:
+                put_l(i, 0)
+                put_l(i, 1)
+                put_h(i, 0)
+                put_h(i, 1)
+            for k in [k for k in range(4, NK) if NSS[k] > 0 and max(1, k - WS) == i]:
+                put("s", ("ws", k), [], widen_s, k, NSS[k])
+            for k in ts[: 1 + (i < 4)]:
+                put_t(k)
+                put_c(k, "s")
+            if i in (QT, QT + 1):
+                put("t", ("qt", i - QT, 0), [], qt, i - QT, 0)
+                put("s", ("qc", i - QT, 0), [("qt", i - QT, 0)], qcp, "s", i - QT, 0)
+            put_l(i, 2)
+            put_l(i, 3)
+            put_h(i, 2)
+            put_h(i, 3)
+            for k in ts[1 + (i < 4) :]:
+                put_t(k)
+                put_c(k, "s")
+            if i in (QT, QT + 1):
+                put("t", ("qt", i - QT, 1), [], qt, i - QT, 1)
+                put("s", ("qc", i - QT, 1), [("qt", i - QT, 1)], qcp, "s", i - QT, 1)
+            if US <= i and UN * (i - US) < 8:
+                for n in range(UN * (i - US), min(8, UN * (i - US + 1))):
+                    put("t", ("u", n), [("qc", n // 4, 0), ("qc", n // 4, 1)], void_logits, (n,))
             if i in (ZS, ZS + 1):
-                class_logits(i - ZS)
+                put("t", ("z", i - ZS), [("qq", i - ZS)], class_logits, i - ZS)
             if i == XS:
-                class_exp(range(8))
-                nc.scalar.activation(out=evoid[:], in_=um[:], func=ACT.Exp)
-            if i >= OS:
-                ready = 3 * ((i - OD) // 3) - 1
-                while next_out < NCHUNK - 1 and NG * next_out + 1 <= ready and len(pending) < 2:
-                    out_mm(next_out, 0, 512)
-                    pending.append(next_out)
-                    next_out += 1
-            if i == NUNIT:
-                while pending or next_out < NCHUNK - 1:
-                    for c in pending:
-                        out_copy("s", c, 0, 512)
-                        store(c, 0, 512)
-                    pending = []
-                    while next_out < NCHUNK - 1 and len(pending) < 2:
-                        out_mm(next_out, 0, 512)
-                        pending.append(next_out)
-                        next_out += 1
-                last = NUNIT - 1
-                for b in range(4):
-                    gain(last, 128 * b, 128 * (b + 1))
-                    if b > 0:
-                        m_quant(last, 128 * (b - 1), 128 * b)
-                        out_mm(NCHUNK - 1, 128 * (b - 1), 128 * b)
-                        out_copy("s", NCHUNK - 1, 128 * (b - 1), 128 * b)
-                    if b == 2:
-                        store(NCHUNK - 1, 0, 256)
-                m_quant(last, 384, 512)
-                out_mm(NCHUNK - 1, 384, 512)
-                out_copy("s", NCHUNK - 1, 384, 512)
-                store(NCHUNK - 1, 256, 512)
+                for k in range(8):
+                    put("s", ("x", k), ["shift", ("z", k // 4)], class_exp, (k,))
+                put("s", "xv", ["shift"], exp_void)
+            for n in range(OUTS.get(i, 0)):
+                put_out(nout)
+                nout += 1
+            for n in range(OCS.get(i, 0)):
+                put_oc(len([x for x in queue["s"] if x[0][0] == "oc"]))
+        while nout < NCHUNK - 1:
+            put_out(nout)
+            nout += 1
+        last = NUNIT - 1
+
+        def put_last(b):
+            n0, n1 = 128 * b, 128 * (b + 1)
+            put("t", ("lo", b), [("lq", b), "sq", ("mq", last - 1)], out_mm, NCHUNK - 1, n0, n1)
+
+        for c in range(len([x for x in queue["s"] if x[0][0] == "oc"]), NCHUNK - 1):
+            put_oc(c)
+        for b in range(4):
+            put("v", ("lm", b), [("h", last, b)], gain, last, 128 * b, 128 * (b + 1))
+            if b > 0:
+                put("v", ("lq", b - 1), [("lm", b - 1)], m_quant, last, 128 * (b - 1), 128 * b)
+        put("v", ("lq", 3), [("lm", 3)], m_quant, last, 384, 512)
+        for b in range(4):
+            put_last(b)
+            put("s", ("lc", b), [("lo", b)], out_copy, "s", NCHUNK - 1, 128 * b, 128 * (b + 1))
+        put("y", "l0", [("lc", 0), ("lc", 1)], store, NCHUNK - 1, 0, 256)
+        put("y", "l1", [("lc", 2), ("lc", 3)], store, NCHUNK - 1, 256, 512)
+
+        made = set()
+        while any(queue.values()):
+            moved = False
+            for eng in queue:
+                while queue[eng] and all(n in made for n in queue[eng][0][1]):
+                    makes, needs, fn, args = queue[eng][0]
+                    queue[eng] = queue[eng][1:]
+                    fn(*args)
+                    made.add(makes)
+                    moved = True
+            assert moved, [q[0][:2] for q in queue.values() if q]

@@ -22,30 +22,37 @@ CHUNK = 512
 NCHUNK = NPIX // CHUNK
 NG = Q // 512
 NUNIT = NCHUNK * NG
-NS1 = 4
-NS2 = 0
-NS = (2,) * 10 + (0,) * 6
-EARLYW = 1
+NS1 = 5
+NS = (0,) * 7 + (2,) * 9
 C2 = "v"
 C3 = "v"
-WLAST = 11
+WLAST = 12
 WL = 10
 QL = 3
 TL = 4
-TR = 3
-WS = 8
+TR = 4
+WS = 6
 VM = 2
 VQ = 1
-QT = 4
-US = 5
-UN = 2
-ZS = 7
+QT = 1
+US = 2
+UN = 1
+ZS = 8
 XS = 11
-OUTS = {13: 1, 14: 1}
-OCS = {14: 2}
+OUTS = {14: 1, 15: 2}
+OCS = {}
 ALT = (2, 3, 4, 5)
 TB = 5
 MB = 15
+VO = 7
+VG = (0, 1)
+NS0 = 3
+NS2 = 4
+NS3 = 0
+W3E = 1
+H1 = 1
+WM = 2
+LB = 2
 
 
 def tile_maskquerysemanticinference_d1p_kernel(
@@ -87,12 +94,11 @@ def tile_maskquerysemanticinference_d1p_kernel(
         load_rows(emb_raw[0], emb_view[0], 1)
         load_pix(0, 1)
         nc.sync.dma_start(out=psc[:, 2:, :], in_=psc_view[:, 2:, :])
+        nc.sync.dma_start(out=pixb[1][:].rearrange("p (h x) -> p h x", h=2), in_=pix_view[1])
         gm_b = const.tile([P, 8], BF16, name="gm_b")
         nc.sync.dma_start(out=gm_b[:].rearrange("p (g t) -> p g t", t=4), in_=g_mask.rearrange("(g p t) -> p g t", p=P, t=4))
         load_rows(emb_raw[1], emb_view[1], 0)
         load_rows(emb_raw[1], emb_view[1], 1)
-        load_pix(1, 0)
-        load_pix(1, 1)
         nc.sync.dma_start(out=pixb[2][:].rearrange("p (h x) -> p h x", h=2), in_=pix_view[2])
         for g in range(NG):
             nc.sync.dma_start(out=q_raw[g][:], in_=q_view[g])
@@ -419,7 +425,7 @@ def tile_maskquerysemanticinference_d1p_kernel(
                 put("s", ("ws", k), [], widen_s, k, n_s)
 
         NK = 2 * NCHUNK
-        NSS = [4, NS1, NS2, NS2] + list(NS[4:])
+        NSS = [NS0, NS1, NS2, NS3] + list(NS[4:])
 
         def put_t(k):
             put("t", ("t", k), ([("wv", k)] if NSS[k] < 8 else []) + ([("ws", k)] if NSS[k] > 0 else []), prep_t, k)
@@ -454,35 +460,41 @@ def tile_maskquerysemanticinference_d1p_kernel(
             put("y", ("st", c), [("oc", c)], store, c, 0, 512)
 
         queue["y"] = []
+        VCOPY = [3 * grp + VO for grp in VG if 4 <= 3 * grp + VO < 2 * NCHUNK]
 
         put("v", "ident_b", [], ident_copy)
-        put_w(0, 4)
+        put_w(0, NS0)
         put("v", ("ec", 0, 0), [("et", 0, 0)], ecp, "v", 0, 0)
         put_q(0)
         put("v", ("eq", 0, 0), [("ec", 0, 0)], eq, 0, 0)
         put("v", ("eq", 0, 1), [("ec", 0, 1)], eq, 0, 1)
         put_c(0, "s")
         put("s", ("ec", 0, 1), [("et", 0, 1)], ecp, "s", 0, 1)
-        put_w(1, NS1)
+        put_w(1, NSS[1])
         put("v", "g2b", [], g2_make)
-        if EARLYW:
-            put_w(2, NS2)
+        put_w(2, NSS[2])
+        if W3E:
+            put_w(3, NSS[3])
         put_c(1, "v")
         put_q(1)
         put("s", ("ec", 1, 0), [("et", 1, 0)], ecp, "s", 1, 0)
         put_h(0, 0)
-        put_h(0, 1)
-        put("s", ("ec", 1, 1), [("et", 1, 1)], ecp, "s", 1, 1)
+        if H1:
+            put_h(0, 1)
         put("v", ("eq", 1, 0), [("ec", 1, 0)], eq, 1, 0)
+        if not W3E:
+            put_w(3, NSS[3])
+        put("s", ("ec", 1, 1), [("et", 1, 1)], ecp, "s", 1, 1)
+        for k in range(4, 4 + WM):
+            put("v", ("wv", k), [], widen_v, k, NSS[k])
         put("v", ("eq", 1, 1), [("ec", 1, 1)], eq, 1, 1)
-        if not EARLYW:
-            put_w(2, NS2)
-        put_w(3, NS2)
+        if not H1:
+            put_h(0, 1)
         put_h(0, 2)
         put_h(0, 3)
         put_c(2, C2)
-        put_c(3, C3)
         put_q(2)
+        put_c(3, C3)
         put_q(3)
         put_t(0)
         for h in range(2):
@@ -512,7 +524,7 @@ def tile_maskquerysemanticinference_d1p_kernel(
         for k in range(4, NK):
             tplan.setdefault(max(1 + (k - 4) // TR, k - TL), []).append(k)
 
-        for k in wplan[0]:
+        for k in wplan[0][WM:]:
             put_w(k, NSS[k]) if NSS[k] == 0 else put("v", ("wv", k), [], widen_v, k, NSS[k])
         for k in qplan.get(0, []):
             put_q(k)
@@ -523,6 +535,9 @@ def tile_maskquerysemanticinference_d1p_kernel(
             put_gain_g(a)
             put_gain(a + 1)
             put_gain(a + 2)
+            kv = 3 * grp + VO
+            if kv in VCOPY:
+                put_c(kv, "v")
             if grp == VM:
                 put("v", "um", [("u", n) for n in range(8)], void_read)
                 for g in range(NG):
@@ -535,6 +550,9 @@ def tile_maskquerysemanticinference_d1p_kernel(
             if grp == VQ:
                 put("v", ("qq", 0), [("qc", 0, 0), ("qc", 0, 1)], qq, 0)
                 put("v", ("qq", 1), [("qc", 1, 0), ("qc", 1, 1)], qq, 1)
+            if grp == 4:
+                for b in range(LB):
+                    put("v", ("lm", b), [("h", NUNIT - 1, b)], gain, NUNIT - 1, 128 * b, 128 * (b + 1))
             put_mq(a + 1)
             put_mq(a + 2)
             if grp == VM + 1:
@@ -554,7 +572,8 @@ def tile_maskquerysemanticinference_d1p_kernel(
                 put("s", ("ws", k), [], widen_s, k, NSS[k])
             for k in ts[: 1 + (i < 4)]:
                 put_t(k)
-                put_c(k, "s")
+                if k not in VCOPY:
+                    put_c(k, "s")
             if i in (QT, QT + 1):
                 put("t", ("qt", i - QT, 0), [], qt, i - QT, 0)
                 put("s", ("qc", i - QT, 0), [("qt", i - QT, 0)], qcp, "s", i - QT, 0)
@@ -564,7 +583,8 @@ def tile_maskquerysemanticinference_d1p_kernel(
             put_h(i, 3)
             for k in ts[1 + (i < 4) :]:
                 put_t(k)
-                put_c(k, "s")
+                if k not in VCOPY:
+                    put_c(k, "s")
             if i in (QT, QT + 1):
                 put("t", ("qt", i - QT, 1), [], qt, i - QT, 1)
                 put("s", ("qc", i - QT, 1), [("qt", i - QT, 1)], qcp, "s", i - QT, 1)
@@ -594,7 +614,8 @@ def tile_maskquerysemanticinference_d1p_kernel(
         for c in range(len([x for x in queue["s"] if x[0][0] == "oc"]), NCHUNK - 1):
             put_oc(c)
         for b in range(4):
-            put("v", ("lm", b), [("h", last, b)], gain, last, 128 * b, 128 * (b + 1))
+            if b >= LB:
+                put("v", ("lm", b), [("h", last, b)], gain, last, 128 * b, 128 * (b + 1))
             if b > 0:
                 put("v", ("lq", b - 1), [("lm", b - 1)], m_quant, last, 128 * (b - 1), 128 * b)
         put("v", ("lq", 3), [("lm", 3)], m_quant, last, 384, 512)

from contextlib import ExitStack

import concourse.mybir as mybir
from concourse.masks import make_identity

Q, D, C, NPIX = 1024, 512, 128, 4096
FLOPS = 2 * Q * D * NPIX + 2 * Q * D * C + 2 * C * Q * NPIX

P = 128
F32 = mybir.dt.float32
BF16 = mybir.dt.bfloat16
I32 = mybir.dt.int32
U32 = mybir.dt.uint32
U8 = mybir.dt.uint8
FP8 = mybir.dt.float8_e4m3fn
FP8X4 = mybir.dt.float8_e4m3fn_x4
ACT = mybir.ActivationFunctionType
ALU = mybir.AluOpType
AX = mybir.AxisListType

CHUNK = 512
NCHUNK = NPIX // CHUNK
NG = Q // 512
NUNIT = NCHUNK * NG
NS1 = 5
NS = (0,) * 7 + (2,) * 9
C2 = "v"
C3 = "v"
WLAST = 12
WL = 10
QL = 3
TL = 4
TR = 4
WS = 6
VM = 2
VQ = 1
QT = 1
US = 2
UN = 1
ZS = 8
XS = 11
OUTS = {14: 1, 15: 2}
OCS = {}
ALT = (2, 3, 4, 5)
TB = 5
MB = 15
VO = 7
VG = (0, 1)
NS0 = 3
NS2 = 4
NS3 = 0
W3E = 1
H1 = 1
WM = 2
LB = 2


def tile_maskquerysemanticinference_d1p_kernel(
    tc, emb, pix_bytes, pix_scale, queries, w_words, w_scales, w_void, g_mask, g_cls, out
):
    nc = tc.nc
    with ExitStack() as ctx:
        const = ctx.enter_context(tc.tile_pool(name="const", bufs=1))
        work = ctx.enter_context(tc.tile_pool(name="work", bufs=1))
        psum = ctx.enter_context(tc.psum_pool(name="psum", bufs=1))

        ident = const.tile([P, P], F32, name="ident")
        make_identity(nc, ident[:])
        ctx.enter_context(tc.manual_schedule())

        warm = const.tile([P, 1], F32, name="warm")
        nc.vector.memset(warm[:], 0.0)
        warm_out = const.tile([P, 1], F32, name="warm_out")
        nc.scalar.activation(out=warm_out[:], in_=warm[:], func=ACT.Exp)

        pixb = [const.tile([P, 4 * 512], U8, name="pixb%d" % c, align_bytes=64) for c in range(NCHUNK)]
        pix_view = pix_bytes.rearrange("(c h p r) k -> c p h (r k)", h=2, p=P, r=2)
        psc = const.tile([P, 2 * NCHUNK, 8], F32, name="psc")
        psc_view = pix_scale.rearrange("(c p r) j -> p c (r j)", p=P, r=2)
        emb_raw = [const.tile([P, 4, 512], BF16, name="emb_raw%d" % g, align_bytes=64) for g in range(NG)]
        emb_view = emb.rearrange("(g p t) k -> g p t k", p=P, t=4)
        q_raw = [const.tile([P, 4, 512], BF16, name="q_raw%d" % g, align_bytes=64) for g in range(NG)]
        q_view = queries.rearrange("(g p t) k -> g p t k", p=P, t=4)

        def load_pix(c, h):
            nc.sync.dma_start(out=pixb[c][:, 1024 * h : 1024 * (h + 1)], in_=pix_view[c][:, h, :])

        def load_rows(tile, view, h):
            nc.sync.dma_start(out=tile[:, 2 * h : 2 * h + 2, :], in_=view[:, 2 * h : 2 * h + 2, :])

        nc.sync.dma_start(out=psc[:, 0:2, :], in_=psc_view[:, 0:2, :])
        load_pix(0, 0)
        load_rows(emb_raw[0], emb_view[0], 0)
        load_rows(emb_raw[0], emb_view[0], 1)
        load_pix(0, 1)
        nc.sync.dma_start(out=psc[:, 2:, :], in_=psc_view[:, 2:, :])
        nc.sync.dma_start(out=pixb[1][:].rearrange("p (h x) -> p h x", h=2), in_=pix_view[1])
        gm_b = const.tile([P, 8], BF16, name="gm_b")
        nc.sync.dma_start(out=gm_b[:].rearrange("p (g t) -> p g t", t=4), in_=g_mask.rearrange("(g p t) -> p g t", p=P, t=4))
        load_rows(emb_raw[1], emb_view[1], 0)
        load_rows(emb_raw[1], emb_view[1], 1)
        nc.sync.dma_start(out=pixb[2][:].rearrange("p (h x) -> p h x", h=2), in_=pix_view[2])
        for g in range(NG):
            nc.sync.dma_start(out=q_raw[g][:], in_=q_view[g])
        w_sc = const.tile([P, C], U8, name="w_sc", align_bytes=64)
        nc.vector.memset(w_sc[:].bitcast(I32), 0)
        for r in range(4):
            nc.sync.dma_start(
                out=w_sc[32 * r : 32 * r + 4, :].bitcast(I32), in_=w_scales[0, 4 * r : 4 * r + 4, :].bitcast(I32)
            )
        w_codes = const.tile([P, 4 * C], U8, name="w_codes", align_bytes=64)
        nc.sync.dma_start(out=w_codes[:].bitcast(I32), in_=w_words[0].rearrange("p n t -> p (n t)").bitcast(I32))
        wv = const.tile([P, 4], BF16, name="wv")
        nc.sync.dma_start(out=wv[:], in_=w_void.rearrange("(p t) -> p t", t=4))
        gc_b = const.tile([P, 8], BF16, name="gc_b")
        nc.sync.dma_start(out=gc_b[:].rearrange("p (g t) -> p g t", t=4), in_=g_cls.rearrange("(g p t) -> p g t", p=P, t=4))
        for c in range(3, NCHUNK):
            nc.sync.dma_start(out=pixb[c][:].rearrange("p (h x) -> p h x", h=2), in_=pix_view[c])

        ident_b = const.tile([P, P], BF16, name="ident_b")
        g2b = const.tile([P, 8], BF16, name="g2b")
        g2s = const.tile([P, 8], F32, name="g2s")
        g2p = psum.tile([P, 512], F32, name="g2p", tag="g2p", bufs=1)

        wides = {}
        pgroup = {}
        pcodes = {}
        psts = {}

        def widen(c, r, j, eng):
            if c not in wides:
                wides[c] = work.tile([P, 4, 512], BF16, name="wide", tag="wide", bufs=5, align_bytes=64)
            src = pixb[c][:, 512 * r + 128 * j : 512 * r + 128 * (j + 1)].bitcast(FP8)
            dst = wides[c][:, r, 128 * j : 128 * (j + 1)]
            scl = psc[:, 2 * c + r // 2, 4 * (r % 2) + j : 4 * (r % 2) + j + 1]
            if eng == "v":
                nc.vector.tensor_scalar(out=dst, in0=src, scalar1=scl, scalar2=None, op0=ALU.mult)
            else:
                nc.scalar.activation(out=dst, in_=src, func=ACT.Copy, scale=scl)

        def transposes(rows, h, tag, bufs):
            bank = psum.tile([P, 512], F32, name="bank_" + tag, tag=tag, bufs=bufs)
            b4 = bank[:].rearrange("p (s u m) -> p s u m", s=2, u=2)
            for s in range(2):
                words = rows[:, 2 * h + s, :].bitcast(F32)
                for u in range(2):
                    nc.tensor.transpose(b4[:, s, u, :], words[:, u::2], ident[:])
            return b4

        def bank_copy(eng, dst, src):
            if eng == "v":
                nc.vector.tensor_copy(out=dst, in_=src)
            else:
                nc.scalar.copy(out=dst, in_=src)

        def stat_group(name):
            return work.tile([P, 2048], BF16, name=name, tag="sgroup", bufs=3, align_bytes=64)

        def stat_copy(eng, grp, h, b4):
            dst = grp[:].bitcast(F32).rearrange("p (s m u) -> p s m u", s=4, u=2)[:, 2 * h : 2 * h + 2]
            bank_copy(eng, dst, b4.rearrange("p s u m -> p s m u"))

        def pix_copy(eng, c, h, b4):
            if c not in pgroup:
                pgroup[c] = work.tile([P, 2048], BF16, name="pgroup", tag="pgroup", bufs=4, align_bytes=64)
            dst = pgroup[c][:].bitcast(F32)[:, 512 * h : 512 * (h + 1)].rearrange("p (m s u) -> p m s u", s=2, u=2)
            bank_copy(eng, dst, b4.rearrange("p s u m -> p m s u"))

        def quant(codes, scales, grp):
            nc.vector.quantize_mx(out=codes.bitcast(FP8X4), scales=scales, in_=grp)

        def pix_quant(c, n0, n1):
            if c not in pcodes:
                pcodes[c] = work.tile([P, 512], U32, name="pcodes", tag="pcodes", bufs=5, align_bytes=64)
                psts[c] = work.tile([P, 512], U8, name="psts", tag="psts", bufs=5, align_bytes=64)
            quant(pcodes[c][:, n0:n1], psts[c][:, n0:n1], pgroup[c][:, 4 * n0 : 4 * n1])

        def mm(o, lc, ls, rc, rs, start=True, stop=True):
            nc.tensor.matmul_mx(
                out=o, lhsT=lc.bitcast(FP8X4), lhsT_scale=ls, rhs=rc.bitcast(FP8X4), rhs_scale=rs, start=start, stop=stop
            )

        ecodes = [const.tile([P, 512], U32, name="ecodes%d" % g, align_bytes=64) for g in range(NG)]
        escales = [const.tile([P, 512], U8, name="escales%d" % g, align_bytes=64) for g in range(NG)]
        qcodes = [const.tile([P, 512], U32, name="qcodes%d" % g, align_bytes=64) for g in range(NG)]
        qscales = [const.tile([P, 512], U8, name="qscales%d" % g, align_bytes=64) for g in range(NG)]
        scodes = [const.tile([P, C], U32, name="scodes%d" % g, align_bytes=64) for g in range(NG)]
        sscales = [const.tile([P, C], U8, name="sscales%d" % g, align_bytes=64) for g in range(NG)]

        lbank = {}
        tanh_t = {}
        mcodes = {}
        mscales = {}
        mtile = {}

        def logits(i, j):
            c, g = divmod(i, NG)
            bank = psum.tile([P, 512], F32, name="lbank", tag="l", bufs=3)
            for t in range(4):
                mm(
                    bank[:, 128 * t : 128 * (t + 1)],
                    ecodes[g][:, 128 * t : 128 * (t + 1)],
                    escales[g][:, 128 * t : 128 * (t + 1)],
                    pcodes[c][:, 128 * j : 128 * (j + 1)],
                    psts[c][:, 128 * j : 128 * (j + 1)],
                )
            lbank[i, j] = bank

        def tanh(i, j):
            if i not in tanh_t:
                tanh_t[i] = work.tile([P, 512, 4], F32, name="tanh", tag="tanh", bufs=TB, align_bytes=64)
            nc.scalar.activation(
                out=tanh_t[i][:, 128 * j : 128 * (j + 1), :],
                in_=lbank[i, j][:].rearrange("p (t n) -> p n t", t=4),
                func=ACT.Tanh,
                scale=0.5,
            )

        def gain(i, n0, n1):
            g = i % NG
            if i not in mtile:
                mtile[i] = work.tile([P, 512, 4], BF16, name="mtile", tag="mtile", bufs=3, align_bytes=64)
            nc.vector.tensor_tensor(
                out=mtile[i][:, n0:n1, :],
                in0=tanh_t[i][:, n0:n1, :],
                in1=g2p[:, 4 * g : 4 * g + 4].unsqueeze(1).broadcast_to([P, n1 - n0, 4]),
                op=ALU.mult,
            )

        def gain_g(i):
            g = i % NG
            mtile[i] = work.tile([P, 512, 4], BF16, name="mtile_g", tag="mtile_g", bufs=1, align_bytes=64)
            nc.gpsimd.tensor_tensor(
                out=mtile[i][:],
                in0=tanh_t[i][:],
                in1=g2s[:, 4 * g : 4 * g + 4].unsqueeze(1).broadcast_to([P, 512, 4]),
                op=ALU.mult,
            )

        def m_quant(i, n0, n1):
            if i not in mcodes:
                mcodes[i] = work.tile([P, 512], U32, name="mcodes", tag="mcodes", bufs=MB, align_bytes=64)
                mscales[i] = work.tile([P, 512], U8, name="mscales", tag="mscales", bufs=MB, align_bytes=64)
            quant(
                mcodes[i][:, n0:n1], mscales[i][:, n0:n1], mtile[i][:, n0:n1, :].rearrange("p n t -> p (n t)")
            )

        obank = {}

        def out_mm(c, n0, n1):
            if c not in obank:
                obank[c] = psum.tile([P, 512], F32, name="obank", tag="o", bufs=3)
            for g in range(NG):
                i = NG * c + g
                mm(
                    obank[c][:, n0:n1], scodes[g][:], sscales[g][:], mcodes[i][:, n0:n1], mscales[i][:, n0:n1],
                    start=(g == 0), stop=(g == NG - 1),
                )

        osb = {}

        def out_copy(eng, c, n0, n1):
            if c not in osb:
                osb[c] = work.tile([P, 512], F32, name="osb", tag="osb", bufs=6)
            bank_copy(eng, osb[c][:, n0:n1], obank[c][:, n0:n1])

        def store(c, n0, n1):
            nc.sync.dma_start(out=out[:, 512 * c + n0 : 512 * c + n1], in_=osb[c][:, n0:n1])

        def widen_half(c, h, n_s):
            for b in range(8):
                r, j = 2 * h + b // 4, b % 4
                widen(c, r, j, "s" if b >= 8 - n_s else "v")

        qg = [None, None]
        def widen_v(k, n_s):
            c, h = divmod(k, 2)
            for b in range(8 - n_s):
                widen(c, 2 * h + b // 4, b % 4, "v")

        def widen_s(k, n_s):
            c, h = divmod(k, 2)
            for b in range(8 - n_s, 8):
                widen(c, 2 * h + b // 4, b % 4, "s")

        prep_bank = {}

        def prep_t(k):
            tag, bufs = ("tr", 1) if k not in ALT else ("o", 3)
            prep_bank[k] = transposes(wides[k // 2], k % 2, tag, bufs)

        def prep_copy(k, eng):
            pix_copy(eng, k // 2, k % 2, prep_bank[k])

        def prep_q(k):
            pix_quant(k // 2, 256 * (k % 2), 256 * (k % 2 + 1))

        zb = [None, None]
        um = const.tile([P, 8], F32, name="um")
        zmx = const.tile([P, 8], F32, name="zmx")
        nmx = const.tile([P, 8], F32, name="nmx")
        esum = const.tile([P, 8], F32, name="esum")
        evoid = const.tile([P, 8], F32, name="evoid")
        mean = const.tile([P, 8], F32, name="mean")
        amp = const.tile([P, 8], F32, name="amp")
        ez = const.tile([P, 8, C], F32, name="ez")
        sgrp = [const.tile([P, C, 4], BF16, name="sgrp%d" % g, align_bytes=64) for g in range(NG)]
        def class_logits(g):
            zb[g] = psum.tile([P, 512], F32, name="zbank", tag="o", bufs=3)
            for t in range(4):
                mm(
                    zb[g][:, 128 * t : 128 * (t + 1)],
                    qcodes[g][:, 128 * t : 128 * (t + 1)],
                    qscales[g][:, 128 * t : 128 * (t + 1)],
                    w_codes[:].bitcast(U32),
                    w_sc[:],
                )

        ubank = {}

        def void_logits(cols):
            if not ubank:
                ubank[0] = psum.tile([P, 512], F32, name="ubank", tag="o", bufs=3)
            for col in cols:
                q4 = qg[col // 4][:].rearrange("p (s m k) -> p s m k", s=4, k=4)
                for k in range(4):
                    nc.tensor.matmul(
                        ubank[0][:, col : col + 1], q4[:, col % 4, :, k], wv[:, k : k + 1], start=(k == 0), stop=(k == 3)
                    )

        def void_read():
            nc.vector.tensor_scalar(out=um[:], in0=ubank[0][:, 0:8], scalar1=6.0, scalar2=None, op0=ALU.add)

        def class_max(g):
            nc.vector.tensor_reduce(
                out=zmx[:, 4 * g : 4 * g + 4],
                in_=zb[g][:].rearrange("p (t c) -> p t c", t=4),
                axis=AX.X,
                op=ALU.max,
            )

        def class_shift():
            nc.vector.tensor_tensor(out=zmx[:], in0=zmx[:], in1=um[:], op=ALU.max)
            nc.vector.tensor_scalar(out=nmx[:], in0=zmx[:], scalar1=-1.0, scalar2=None, op0=ALU.mult)
            nc.vector.tensor_tensor(out=um[:], in0=um[:], in1=zmx[:], op=ALU.subtract)

        def class_exp(ks):
            for k in ks:
                nc.scalar.activation(
                    out=ez[:, k, :],
                    in_=zb[k // 4][:, 128 * (k % 4) : 128 * (k % 4 + 1)],
                    func=ACT.Exp,
                    bias=nmx[:, k : k + 1],
                    scale=1.0,
                    accum_out=esum[:, k : k + 1],
                )

        def class_factors():
            nc.vector.tensor_tensor(out=evoid[:], in0=evoid[:], in1=esum[:], op=ALU.add)
            nc.vector.tensor_scalar(out=mean[:], in0=esum[:], scalar1=1.0 / C, scalar2=None, op0=ALU.mult)
            nc.vector.reciprocal(out=evoid[:], in_=evoid[:])
            nc.vector.tensor_tensor(out=amp[:], in0=evoid[:], in1=gc_b[:], op=ALU.mult)

        def class_scores():
            for k in range(8):
                nc.vector.tensor_scalar(
                    out=sgrp[k // 4][:, :, k % 4],
                    in0=ez[:, k, :],
                    scalar1=mean[:, k : k + 1],
                    scalar2=amp[:, k : k + 1],
                    op0=ALU.subtract,
                    op1=ALU.mult,
                )
            for g in range(NG):
                quant(scodes[g][:], sscales[g][:], sgrp[g][:].rearrange("p c t -> p (c t)"))


        queue = {"t": [], "s": [], "v": [], "g": []}

        def put(eng, makes, needs, fn, *args):
            queue[eng].append((makes, needs, fn, args))

        eg = [stat_group("eg0"), stat_group("eg1")]
        ebank = {}

        def et(g, h):
            ebank[g, h] = transposes(emb_raw[g], h, "o", 3)

        def ecp(eng, g, h):
            stat_copy(eng, eg[g], h, ebank[g, h])

        def eq(g, h):
            quant(ecodes[g][:, 256 * h : 256 * h + 256], escales[g][:, 256 * h : 256 * h + 256], eg[g][:, 1024 * h : 1024 * h + 1024])

        def qt(g, h):
            if h == 0:
                qg[g] = stat_group("qg%d" % g)
            ebank[g + 2, h] = transposes(q_raw[g], h, "o", 3)

        def qcp(eng, g, h):
            stat_copy(eng, qg[g], h, ebank[g + 2, h])

        def qq(g):
            quant(qcodes[g][:], qscales[g][:], qg[g][:])

        def g2_make():
            nc.vector.tensor_scalar(out=g2b[:], in0=gm_b[:], scalar1=0.5, scalar2=None, op0=ALU.mult)

        def g2_bank():
            nc.tensor.matmul(g2p[:, 0:8], ident_b[:], g2b[:], start=True, stop=True)

        def g2_sbuf():
            nc.vector.tensor_scalar(out=g2s[:], in0=gm_b[:], scalar1=0.5, scalar2=None, op0=ALU.mult)

        def exp_void():
            nc.scalar.activation(out=evoid[:], in_=um[:], func=ACT.Exp)

        def ident_copy():
            nc.vector.tensor_copy(out=ident_b[:], in_=ident[:])

        def put_w(k, n_s):
            if n_s < 8:
                put("v", ("wv", k), [], widen_v, k, n_s)
            if n_s > 0:
                put("s", ("ws", k), [], widen_s, k, n_s)

        NK = 2 * NCHUNK
        NSS = [NS0, NS1, NS2, NS3] + list(NS[4:])

        def put_t(k):
            put("t", ("t", k), ([("wv", k)] if NSS[k] < 8 else []) + ([("ws", k)] if NSS[k] > 0 else []), prep_t, k)

        def put_c(k, eng):
            put(eng, ("c", k), [("t", k)], prep_copy, k, eng)

        def put_q(k):
            put("v", ("q", k), [("c", k)], prep_q, k)

        def put_l(i, j):
            c, g = divmod(i, NG)
            put("t", ("l", i, j), [("q", 2 * c + j // 2), ("eq", g, 0), ("eq", g, 1)], logits, i, j)

        def put_h(i, j):
            put("s", ("h", i, j), [("l", i, j)], tanh, i, j)

        def put_gain(i):
            put("v", ("m", i), [("h", i, j) for j in range(4)] + ["g2p"], gain, i, 0, 512)

        def put_gain_g(i):
            put("g", ("m", i), [("h", i, j) for j in range(4)] + ["g2s"], gain_g, i)

        def put_mq(i):
            put("v", ("mq", i), [("m", i)], m_quant, i, 0, 512)

        def put_out(c):
            put("t", ("o", c), ["sq", ("mq", 2 * c), ("mq", 2 * c + 1)], out_mm, c, 0, 512)

        def put_oc(c, eng="s"):
            put(eng, ("oc", c), [("o", c)], out_copy, eng, c, 0, 512)
            put("y", ("st", c), [("oc", c)], store, c, 0, 512)

        queue["y"] = []
        VCOPY = [3 * grp + VO for grp in VG if 4 <= 3 * grp + VO < 2 * NCHUNK]

        put("v", "ident_b", [], ident_copy)
        put_w(0, NS0)
        put("v", ("ec", 0, 0), [("et", 0, 0)], ecp, "v", 0, 0)
        put_q(0)
        put("v", ("eq", 0, 0), [("ec", 0, 0)], eq, 0, 0)
        put("v", ("eq", 0, 1), [("ec", 0, 1)], eq, 0, 1)
        put_c(0, "s")
        put("s", ("ec", 0, 1), [("et", 0, 1)], ecp, "s", 0, 1)
        put_w(1, NSS[1])
        put("v", "g2b", [], g2_make)
        put_w(2, NSS[2])
        if W3E:
            put_w(3, NSS[3])
        put_c(1, "v")
        put_q(1)
        put("s", ("ec", 1, 0), [("et", 1, 0)], ecp, "s", 1, 0)
        put_h(0, 0)
        if H1:
            put_h(0, 1)
        put("v", ("eq", 1, 0), [("ec", 1, 0)], eq, 1, 0)
        if not W3E:
            put_w(3, NSS[3])
        put("s", ("ec", 1, 1), [("et", 1, 1)], ecp, "s", 1, 1)
        for k in range(4, 4 + WM):
            put("v", ("wv", k), [], widen_v, k, NSS[k])
        put("v", ("eq", 1, 1), [("ec", 1, 1)], eq, 1, 1)
        if not H1:
            put_h(0, 1)
        put_h(0, 2)
        put_h(0, 3)
        put_c(2, C2)
        put_q(2)
        put_c(3, C3)
        put_q(3)
        put_t(0)
        for h in range(2):
            put("t", ("et", 0, h), [], et, 0, h)
        put_l(0, 0)
        put_l(0, 1)
        put_t(1)
        for h in range(2):
            put("t", ("et", 1, h), [], et, 1, h)
        put_l(0, 2)
        put_l(0, 3)
        put_t(2)
        put("t", "g2p", ["g2b", "ident_b"], g2_bank)
        put_l(1, 0)
        put_l(1, 1)
        put_t(3)
        put_h(1, 0)
        put_h(1, 1)

        wplan = {}
        for k in range(4, NK):
            wplan.setdefault(0 if k <= WLAST else max(1, (k - WL) // 3), []).append(k)
        qplan = {}
        for k in range(4, NK):
            qplan.setdefault(max(0, (k - QL) // 3), []).append(k)
        tplan = {}
        for k in range(4, NK):
            tplan.setdefault(max(1 + (k - 4) // TR, k - TL), []).append(k)

        for k in wplan[0][WM:]:
            put_w(k, NSS[k]) if NSS[k] == 0 else put("v", ("wv", k), [], widen_v, k, NSS[k])
        for k in qplan.get(0, []):
            put_q(k)
        for grp in range(5):
            a = 3 * grp
            if grp == 0:
                put("v", "g2s", [], g2_sbuf)
            put_gain_g(a)
            put_gain(a + 1)
            put_gain(a + 2)
            kv = 3 * grp + VO
            if kv in VCOPY:
                put_c(kv, "v")
            if grp == VM:
                put("v", "um", [("u", n) for n in range(8)], void_read)
                for g in range(NG):
                    put("v", ("zm", g), [("z", g)], class_max, g)
                put("v", "shift", ["um", ("zm", 0), ("zm", 1)], class_shift)
            if grp == VM + 1:
                put("v", "fac", [("x", k) for k in range(8)] + ["xv"], class_factors)
            for k in wplan.get(grp + 1, []):
                put("v", ("wv", k), [], widen_v, k, NSS[k])
            if grp == VQ:
                put("v", ("qq", 0), [("qc", 0, 0), ("qc", 0, 1)], qq, 0)
                put("v", ("qq", 1), [("qc", 1, 0), ("qc", 1, 1)], qq, 1)
            if grp == 4:
                for b in range(LB):
                    put("v", ("lm", b), [("h", NUNIT - 1, b)], gain, NUNIT - 1, 128 * b, 128 * (b + 1))
            put_mq(a + 1)
            put_mq(a + 2)
            if grp == VM + 1:
                put("v", "sq", ["fac"], class_scores)
            for k in qplan.get(grp + 1, []):
                put_q(k)
            put_mq(a)
        nout = 0
        for i in range(1, NUNIT):
            ts = tplan.get(i, [])
            if i > 1:
                put_l(i, 0)
                put_l(i, 1)
                put_h(i, 0)
                put_h(i, 1)
            for k in [k for k in range(4, NK) if NSS[k] > 0 and max(1, k - WS) == i]:
                put("s", ("ws", k), [], widen_s, k, NSS[k])
            for k in ts[: 1 + (i < 4)]:
                put_t(k)
                if k not in VCOPY:
                    put_c(k, "s")
            if i in (QT, QT + 1):
                put("t", ("qt", i - QT, 0), [], qt, i - QT, 0)
                put("s", ("qc", i - QT, 0), [("qt", i - QT, 0)], qcp, "s", i - QT, 0)
            put_l(i, 2)
            put_l(i, 3)
            put_h(i, 2)
            put_h(i, 3)
            for k in ts[1 + (i < 4) :]:
                put_t(k)
                if k not in VCOPY:
                    put_c(k, "s")
            if i in (QT, QT + 1):
                put("t", ("qt", i - QT, 1), [], qt, i - QT, 1)
                put("s", ("qc", i - QT, 1), [("qt", i - QT, 1)], qcp, "s", i - QT, 1)
            if US <= i and UN * (i - US) < 8:
                for n in range(UN * (i - US), min(8, UN * (i - US + 1))):
                    put("t", ("u", n), [("qc", n // 4, 0), ("qc", n // 4, 1)], void_logits, (n,))
            if i in (ZS, ZS + 1):
                put("t", ("z", i - ZS), [("qq", i - ZS)], class_logits, i - ZS)
            if i == XS:
                for k in range(8):
                    put("s", ("x", k), ["shift", ("z", k // 4)], class_exp, (k,))
                put("s", "xv", ["shift"], exp_void)
            for n in range(OUTS.get(i, 0)):
                put_out(nout)
                nout += 1
            for n in range(OCS.get(i, 0)):
                put_oc(len([x for x in queue["s"] if x[0][0] == "oc"]))
        while nout < NCHUNK - 1:
            put_out(nout)
            nout += 1
        last = NUNIT - 1

        def put_last(b):
            n0, n1 = 128 * b, 128 * (b + 1)
            put("t", ("lo", b), [("lq", b), "sq", ("mq", last - 1)], out_mm, NCHUNK - 1, n0, n1)

        for c in range(len([x for x in queue["s"] if x[0][0] == "oc"]), NCHUNK - 1):
            put_oc(c)
        for b in range(4):
            if b >= LB:
                put("v", ("lm", b), [("h", last, b)], gain, last, 128 * b, 128 * (b + 1))
            if b > 0:
                put("v", ("lq", b - 1), [("lm", b - 1)], m_quant, last, 128 * (b - 1), 128 * b)
        put("v", ("lq", 3), [("lm", 3)], m_quant, last, 384, 512)
        for b in range(4):
            put_last(b)
            put("s", ("lc", b), [("lo", b)], out_copy, "s", NCHUNK - 1, 128 * b, 128 * (b + 1))
        put("y", "l0", [("lc", 0), ("lc", 1)], store, NCHUNK - 1, 0, 256)
        put("y", "l1", [("lc", 2), ("lc", 3)], store, NCHUNK - 1, 256, 512)

        made = set()
        while any(queue.values()):
            moved = False
            for eng in queue:
                while queue[eng] and all(n in made for n in queue[eng][0][1]):
                    makes, needs, fn, args = queue[eng][0]
                    queue[eng] = queue[eng][1:]
                    fn(*args)
                    made.add(makes)
                    moved = True
            assert moved, [q[0][:2] for q in queue.values() if q]
